import numpy as np, ml_dtypes
CORES = [33,161,289,417,57,185,313,441]
N = 8
import mx_ref
NC, ROOT = 128, 4
BF = ml_dtypes.bfloat16
def cut(t, i, w=512):
    return t[:, w * i:w * i + w]
def term(a, B):
    return np.stack([np.maximum(mx_ref.matmul(mx_ref.quantize(cut(a, i)), B), 0) for i in range(4)], axis=2).reshape(128, -1)
def setup_inputs(rng):
    def f(*shape):
        return mx_ref.flush((rng.standard_normal(shape, dtype=np.float32) * np.exp2(rng.integers(-2, 3, shape[:-1] + (1,)))).astype(BF))
    return {"a": f(N, 128, 4 * 512), "b": f(N, 128, 4 * NC)}
def setup_inputs_blocks(rng):
    d = setup_inputs(rng)
    for k in ("a", "b"): d[k] = mx_ref.spread(d[k], rng, 2)
    return d
def setup_inputs_wide(rng):
    d = setup_inputs(rng)
    for k in ("a", "b"): d[k] = mx_ref.flush((d[k].astype(np.float32) * np.exp2(rng.integers(-4, 5, (N, 1, 1))).astype(np.float32)).astype(BF))
    return d
def setup_inputs_lossless(rng):
    a = np.zeros((N, 128, 4 * 128, 4), np.float32)
    for r in range(N):
        k = rng.integers(0, 512, size=4 * 128)
        a[r, k // 4, np.arange(4 * 128), k % 4] = 1.0
    size = np.repeat(2.0 ** rng.integers(-4, 5, size=(1, 1, (4 * NC) // 4)), 4, axis=2)
    b = (rng.random((N, 128, 4 * NC)) < 0.8) * size
    return {"a": a.reshape(N, 128, 4 * 512).astype(BF), "b": b.astype(np.float32).astype(BF)}
def reference(a, b):
    B0 = mx_ref.quantize(b[ROOT])
    T = [term(a[r], B0) for r in range(N)]
    y = np.zeros((N, 128, 4 * NC), np.float32)
    y[:] = mx_ref.total(T)
    return {"y": y}

@@ -1,0 +1,243 @@
+from concourse.bass import DstId, RemoteDMATransfer
+from concourse.mybir import dt, AluOpType, ActivationFunctionType
+
+W = 128
+E = 512
+SCRATCH = {
+    "bt": ("sbuf", [128, E], "bfloat16"),
+    "at": ("sbuf", [128, 4 * E], "bfloat16"),
+    "qa": ("sbuf", [128, 4 * W], "float8_e4m3fn_x4"),
+    "sa": ("sbuf", [128, 4 * W], "uint8"),
+    "qb": ("sbuf", [128, W], "float8_e4m3fn_x4"),
+    "sb": ("sbuf", [128, W], "uint8"),
+    "wt": ("sbuf", [128, 4 * E], "bfloat16"),
+    "qw": ("sbuf", [128, 4 * W], "float8_e4m3fn_x4"),
+    "sw": ("sbuf", [128, 4 * W], "uint8"),
+    "ht": ("sbuf", [128, E], "bfloat16"),
+    "qh": ("sbuf", [128, W], "float8_e4m3fn_x4"),
+    "sh": ("sbuf", [128, W], "uint8"),
+    "ql": ("sbuf", [128, 4 * W], "float8_e4m3fn_x4"),
+    "sl": ("sbuf", [128, 4 * W], "uint8"),
+    "yt": ("sbuf", [128, E], "float32"),
+    "pt": ("psum", [128, 2048], "float32"),
+    "ps": ("psum", [128, 2048], "float32"),
+}
+SEMAPHORES = (["ldb", "lda", "zed", "dia", "selq", "aq", "bq", "relu", "hq", "cp", "st", "sent", "inb"]
+              + ["in%d" % s for s in range(4)] + ["tm%d" % b for b in range(4)] + ["sm%d" % b for b in range(4)])
+_PLAN = {}
+
+
+def _plan(T, topo):
+    if _PLAN:
+        return _PLAN
+    cores, root = list(T.cores), T.cores[T.root]
+    place = {}
+    for k in range(512):
+        place.setdefault((topo.host(k), topo.chip(k)), []).append(k)
+
+    def cross(c):
+        return [d for d in cores if d != c and topo.host(d) == topo.host(c)][0]
+
+    def rack(c):
+        return topo.rack(topo.host(c))
+
+    def plane(c):
+        return [d for d in cores if d != c and topo.chip(d) == topo.chip(c) and rack(d) == rack(c)][0]
+
+    def cable(c):
+        return [d for d in cores if topo.chip(d) == topo.chip(c) and rack(d) != rack(c) and topo.may_write(c, d)][0]
+
+    def helper(c, same_die):
+        return [k for k in place[(topo.host(c), topo.chip(c))] if k != c and topo.may_write(k, cross(c))
+                and (topo.die(k) == topo.die(c)) == same_die][0]
+
+    sends, gathers = {}, {}
+
+    def send(core, held, slot, dsts):
+        sends.setdefault(core, []).append((held, slot, dsts))
+
+    far, near = cross(root), root
+    far2, near2 = cable(far), cable(near)
+    x0, x1, x3 = helper(near, True), helper(plane(near), True), helper(near2, True)
+    send(root, "B", "B", [x0, x3])
+    send(root, "B", "B", [plane(root)])
+    send(x0, "B", "B", [far, plane(far)])
+    send(x3, "B", "B", [far2, plane(far2), near2])
+    send(plane(root), "B", "B", [cable(plane(root))])
+    summing = {}
+    for c in (far, plane(far), far2, plane(far2)):
+        summing[c] = helper(c, True)
+    for c in (near2, plane(near2)):
+        summing[c] = helper(c, False)
+    both = [summing[far], summing[plane(far)]]
+    send(root, "own", 0, [x0])
+    send(x0, 0, 0, both)
+    send(plane(root), "own", 1, [x1])
+    send(x1, 1, 1, both)
+    for base, first in ((far, 2), (far2, 0), (near2, 0)):
+        for i, c in enumerate((base, plane(base))):
+            send(c, "own", first + i, [summing[c], summing[plane(c)]])
+    for c in summing:
+        gathers[summing[c]] = [0, 2, 3, 1] if rack(c) == rack(root) else [0, 1]
+    for c in summing:
+        slot = 0 if rack(c) == rack(root) else (1 if topo.chip(c) == topo.chip(far) else 2)
+        send(summing[c], "own", slot, [c, cross(c), cable(c), cross(cable(c))])
+    for c in cores:
+        gathers[c] = [0, 1, 2] if rack(c) == rack(root) else [1, 2, 0]
+    off = {}
+
+    def engines(src, dst):
+        m = topo.mask(src, dst)
+        if (topo.host(src), topo.chip(src)) == (topo.host(dst), topo.chip(dst)):
+            if src not in off:
+                off[src] = [topo.mask(src, d) for d in cores if (topo.host(d), topo.chip(d)) != (topo.host(src), topo.chip(src))
+                            and topo.may_write(src, d)][0]
+            m = m & ~off[src]
+        return m
+
+    arrive = {}
+    for s in sends:
+        for held, slot, dsts in sends[s]:
+            for d in dsts:
+                arrive[(d, slot)] = 2 * bin(engines(s, d)).count("1")
+    _PLAN.update(root=root, sends=sends, gathers=gathers, engines=engines, arrive=arrive,
+                 summing=set(summing.values()))
+    return _PLAN
+
+
+def rank_program(g, core, T, topo):
+    plan = _plan(T, topo)
+    rank = T.rank_of(core)
+    sends = plan["sends"].get(core, [])
+    is_root, sums = core == plan["root"], core in plan["summing"]
+    if rank is None and not sends:
+        return
+    sent = [0]
+
+    def slot_views(slot):
+        if slot == "B":
+            return T.qb[:], T.sb[:], T.sem.inb
+        return T.ql[:, W * slot:W * slot + W], T.sl[:, W * slot:W * slot + W], T.sem["in%d" % slot]
+
+    def do_send(held, slot, dsts):
+        if held == "own":
+            codes, scales = T.qh[:], T.sh[:]
+        else:
+            codes, scales = slot_views(held)[:2]
+        dcodes, dscales, sem = slot_views(slot)
+        by_mask = {}
+        for d in dsts:
+            by_mask.setdefault(plan["engines"](core, d), []).append(d)
+        for src, dst in ((codes.bitcast(dt.uint8), dcodes.bitcast(dt.uint8)), (scales, dscales)):
+            transfers = []
+            for m in by_mask:
+                ids = []
+                for d in by_mask[m]:
+                    rid, pid = topo.addr(d, core)
+                    ids.append(DstId(rid=rid, pnc=pid))
+                transfers.append(RemoteDMATransfer(dst_ids=ids, dma_engine_mask=m, remote_sem=sem,
+                                                   srcs=[src], dsts=[dst for d in ids]))
+                sent[0] += bin(m).count("1")
+            g.remote_dma_fused(transfers, local_sem=T.sem.sent)
+
+    def selections_zero():
+        g.vector.memset(T.wt[:], 0.0).then_inc(T.sem.zed, 1)
+
+    def selections_ones():
+        g.wait_ge(T.sem.zed, 1)
+        for b in range(4):
+            v = T.wt[:, E * b + b:E * b + E:4]
+            g.affine_select(v, v, [[-1, W]], AluOpType.not_equal, 1.0, 0, 1).then_inc(T.sem.dia, 1)
+
+    def selections_quantise():
+        g.vector.wait_ge(T.sem.dia, 4)
+        g.vector.quantize_mx(T.qw[:], T.sw[:], T.wt[:]).then_inc(T.sem.selq, 1)
+
+    def bank(buf, b):
+        return buf[:, 512 * b:512 * b + W]
+
+    def drain(buf, mm, out, relu, done):
+        for b in (0, 2):
+            g.vector.wait_ge(T.sem["%s%d" % (mm, b)], 1)
+            v = out[:, b:E:4]
+            if relu:
+                g.vector.tensor_scalar(v, bank(buf, b), 0.0, None, AluOpType.max).then_inc(done, 1)
+            else:
+                g.vector.tensor_copy(v, bank(buf, b)).then_inc(done, 1)
+        for b in (1, 3):
+            g.scalar.wait_ge(T.sem["%s%d" % (mm, b)], 1)
+            func = ActivationFunctionType.Relu if relu else ActivationFunctionType.Copy
+            g.scalar.activation(out[:, b:E:4], bank(buf, b), func).then_inc(done, 1)
+
+    def quantise_own(done):
+        g.vector.wait_ge(done, 4)
+        g.vector.quantize_mx(T.qh[:], T.sh[:], T.ht[:]).then_inc(T.sem.hq, 1)
+
+    if is_root:
+        g.sync.dma_start(T.bt[:], T.b[:]).then_inc(T.sem.ldb, 16)
+    if rank is not None:
+        g.sync.dma_start(T.at[:], T.a[:]).then_inc(T.sem.lda, 16)
+
+    unpacks = rank is not None or sums
+    if unpacks:
+        selections_zero()
+        if not is_root:
+            selections_ones()
+            selections_quantise()
+
+    waited = set()
+    for held, slot, dsts in sends:
+        if held not in waited:
+            waited.add(held)
+            if held == "own":
+                if is_root:
+                    selections_ones()
+                g.wait_ge(T.sem.hq, 1)
+            elif held == "B" and is_root:
+                g.wait_ge(T.sem.bq, 1)
+            else:
+                g.wait_ge(slot_views(held)[2], plan["arrive"][(core, held)])
+        do_send(held, slot, dsts)
+
+    if rank is not None:
+        if is_root:
+            g.vector.wait_ge(T.sem.ldb, 16)
+            g.vector.quantize_mx(T.qb[:], T.sb[:], T.bt[:]).then_inc(T.sem.bq, 1)
+        g.vector.wait_ge(T.sem.lda, 16)
+        g.vector.quantize_mx(T.qa[:], T.sa[:], T.at[:]).then_inc(T.sem.aq, 1)
+        g.tensor.wait_ge(T.sem.aq, 1)
+        if is_root:
+            g.tensor.wait_ge(T.sem.bq, 1)
+        else:
+            g.tensor.wait_ge(T.sem.inb, plan["arrive"][(core, "B")])
+        for i in range(4):
+            part = slice(W * i, W * i + W)
+            g.tensor.matmul_mx(bank(T.pt, i), T.qa[:, part], T.sa[:, part], T.qb[:], T.sb[:], True, True
+                               ).then_inc(T.sem["tm%d" % i], 1)
+        drain(T.pt, "tm", T.ht, True, T.sem.relu)
+        quantise_own(T.sem.relu)
+        if is_root:
+            selections_quantise()
+
+    if unpacks:
+        g.tensor.wait_ge(T.sem.selq, 1)
+        slots = plan["gathers"][core]
+        for s in slots:
+            codes, scales, sem = slot_views(s)
+            g.tensor.wait_ge(sem, plan["arrive"][(core, s)])
+            for b in range(4):
+                part = slice(W * b, W * b + W)
+                mm = g.tensor.matmul_mx(bank(T.ps, b), T.qw[:, part], T.sw[:, part], codes, scales,
+                                        s == slots[0], s == slots[-1])
+                if s == slots[-1]:
+                    mm.then_inc(T.sem["sm%d" % b], 1)
+        if sums:
+            drain(T.ps, "sm", T.ht, False, T.sem.cp)
+            quantise_own(T.sem.cp)
+        else:
+            drain(T.ps, "sm", T.yt, False, T.sem.cp)
+            g.sync.wait_ge(T.sem.cp, 4)
+            g.sync.dma_start(T.y[:], T.yt[:]).then_inc(T.sem.st, 16)
+            g.sync.wait_ge(T.sem.st, 16)
+    if sent[0]:
+        g.wait_ge(T.sem.sent, sent[0])

@@ -22,7 +22,7 @@ SCRATCH = {
     "pt": ("psum", [128, 2048], "float32"),
     "ps": ("psum", [128, 2048], "float32"),
 }
-SEMAPHORES = (["ldb", "lda", "zed", "dia", "selq", "aq", "bq", "relu", "hq", "cp", "st", "sent", "inb"]
+SEMAPHORES = (["ldb", "lda", "zed", "dia", "selq", "aq", "bq", "relu", "hq", "cp", "st", "sent", "inb", "scb", "sc0", "sc1"]
               + ["in%d" % s for s in range(4)] + ["tm%d" % b for b in range(4)] + ["sm%d" % b for b in range(4)])
 _PLAN = {}
 
@@ -51,18 +51,40 @@ def _plan(T, topo):
         return [k for k in place[(topo.host(c), topo.chip(c))] if k != c and topo.may_write(k, cross(c))
                 and (topo.die(k) == topo.die(c)) == same_die][0]
 
+    def on_chip(src, dst):
+        return (topo.host(src), topo.chip(src)) == (topo.host(dst), topo.chip(dst))
+
+    def bits(m):
+        return [1 << e for e in range(m.bit_length()) if m >> e & 1]
+
+    def engines(src, dsts, apart):
+        off = [d for d in dsts if not on_chip(src, d)]
+        leaves = [topo.mask(src, d) for d in cores if not on_chip(src, d) and topo.may_write(src, d)][0]
+        by = {}
+        for d in dsts:
+            if on_chip(src, d):
+                m = topo.mask(src, d) & ~leaves
+                if len(off) > 1 and not apart:
+                    m = sum(bits(m)[::2])
+            else:
+                m = topo.mask(src, d)
+                if apart:
+                    share = len(bits(m)) // len(off)
+                    m = sum(bits(m)[share * off.index(d):share * off.index(d) + share])
+            by.setdefault(m, []).append(d)
+        return by
+
     sends, gathers = {}, {}
 
-    def send(core, held, slot, dsts):
-        sends.setdefault(core, []).append((held, slot, dsts))
+    def send(core, held, slot, dsts, apart=False):
+        sends.setdefault(core, []).append((held, slot, engines(core, dsts, apart)))
 
     far, near = cross(root), root
     far2, near2 = cable(far), cable(near)
-    x0, x1, x3 = helper(near, True), helper(plane(near), True), helper(near2, True)
-    send(root, "B", "B", [x0, x3])
-    send(root, "B", "B", [plane(root)])
+    x0, x1, x2 = helper(near, True), helper(plane(near), True), helper(near2, True)
+    send(root, "B", "B", [x0, x2, plane(root)], apart=True)
     send(x0, "B", "B", [far, plane(far)])
-    send(x3, "B", "B", [far2, plane(far2), near2])
+    send(x2, "B", "B", [far2, plane(far2), near2])
     send(plane(root), "B", "B", [cable(plane(root))])
     summing = {}
     for c in (far, plane(far), far2, plane(far2)):
@@ -70,38 +92,29 @@ def _plan(T, topo):
     for c in (near2, plane(near2)):
         summing[c] = helper(c, False)
     both = [summing[far], summing[plane(far)]]
-    send(root, "own", 0, [x0])
-    send(x0, 0, 0, both)
-    send(plane(root), "own", 1, [x1])
-    send(x1, 1, 1, both)
-    for base, first in ((far, 2), (far2, 0), (near2, 0)):
-        for i, c in enumerate((base, plane(base))):
-            send(c, "own", first + i, [summing[c], summing[plane(c)]])
-    for c in summing:
-        gathers[summing[c]] = [0, 2, 3, 1] if rack(c) == rack(root) else [0, 1]
+    for slot, c, x in ((0, root, x0), (1, plane(root), x1)):
+        send(c, "own", slot, [x])
+        send(x, slot, slot, both)
+    for base in (far, far2, near2):
+        for c, own, other in ((base, 2, 3), (plane(base), 3, 2)):
+            send(c, "own", own, [summing[c], summing[plane(c)]])
+            gathers[summing[c]] = [0, own, other, 1] if base == far else [own, other]
     for c in summing:
         slot = 0 if rack(c) == rack(root) else (1 if topo.chip(c) == topo.chip(far) else 2)
         send(summing[c], "own", slot, [c, cross(c), cable(c), cross(cable(c))])
     for c in cores:
-        gathers[c] = [0, 1, 2] if rack(c) == rack(root) else [1, 2, 0]
-    off = {}
+        side = [1, 2] if topo.chip(c) == topo.chip(far) else [2, 1]
+        gathers[c] = [0] + side if rack(c) == rack(root) else side + [0]
 
-    def engines(src, dst):
-        m = topo.mask(src, dst)
-        if (topo.host(src), topo.chip(src)) == (topo.host(dst), topo.chip(dst)):
-            if src not in off:
-                off[src] = [topo.mask(src, d) for d in cores if (topo.host(d), topo.chip(d)) != (topo.host(src), topo.chip(src))
-                            and topo.may_write(src, d)][0]
-            m = m & ~off[src]
-        return m
-
-    arrive = {}
+    arrive, split = {}, set()
     for s in sends:
-        for held, slot, dsts in sends[s]:
-            for d in dsts:
-                arrive[(d, slot)] = 2 * bin(engines(s, d)).count("1")
-    _PLAN.update(root=root, sends=sends, gathers=gathers, engines=engines, arrive=arrive,
-                 summing=set(summing.values()))
+        for held, slot, by in sends[s]:
+            if held != "own" and s != root:
+                split.add((s, held))
+            for m in by:
+                for d in by[m]:
+                    arrive[(d, slot)] = len(bits(m))
+    _PLAN.update(root=root, sends=sends, gathers=gathers, arrive=arrive, split=split, summing=set(summing.values()))
     return _PLAN
 
 
@@ -116,25 +129,39 @@ def rank_program(g, core, T, topo):
 
     def slot_views(slot):
         if slot == "B":
-            return T.qb[:], T.sb[:], T.sem.inb
-        return T.ql[:, W * slot:W * slot + W], T.sl[:, W * slot:W * slot + W], T.sem["in%d" % slot]
+            return T.qb[:], T.sb[:]
+        return T.ql[:, W * slot:W * slot + W], T.sl[:, W * slot:W * slot + W]
 
-    def do_send(held, slot, dsts):
+    def slot_sems(c, slot):
+        name = str(slot).lower()
+        codes = T.sem["in" + name]
+        return codes, (T.sem["sc" + name] if (c, slot) in plan["split"] else codes)
+
+    def wait_tile(queue, slot):
+        n = plan["arrive"][(core, slot)]
+        codes, scales = slot_sems(core, slot)
+        if (core, slot) in plan["split"]:
+            queue.wait_ge(scales, n)
+            queue.wait_ge(codes, n)
+        else:
+            queue.wait_ge(codes, 2 * n)
+
+    def do_send(held, slot, by):
         if held == "own":
             codes, scales = T.qh[:], T.sh[:]
         else:
-            codes, scales = slot_views(held)[:2]
-        dcodes, dscales, sem = slot_views(slot)
-        by_mask = {}
-        for d in dsts:
-            by_mask.setdefault(plan["engines"](core, d), []).append(d)
-        for src, dst in ((codes.bitcast(dt.uint8), dcodes.bitcast(dt.uint8)), (scales, dscales)):
+            codes, scales = slot_views(held)
+        dcodes, dscales = slot_views(slot)
+        for src, dst, which in ((scales, dscales, 1), (codes.bitcast(dt.uint8), dcodes.bitcast(dt.uint8), 0)):
+            if (core, held) in plan["split"]:
+                g.wait_ge(slot_sems(core, held)[which], plan["arrive"][(core, held)])
             transfers = []
-            for m in by_mask:
+            for m in by:
                 ids = []
-                for d in by_mask[m]:
+                for d in by[m]:
                     rid, pid = topo.addr(d, core)
                     ids.append(DstId(rid=rid, pnc=pid))
+                sem = slot_sems(by[m][0], slot)[which]
                 transfers.append(RemoteDMATransfer(dst_ids=ids, dma_engine_mask=m, remote_sem=sem,
                                                    srcs=[src], dsts=[dst for d in ids]))
                 sent[0] += bin(m).count("1")
@@ -185,19 +212,14 @@ def rank_program(g, core, T, topo):
             selections_ones()
             selections_quantise()
 
-    waited = set()
-    for held, slot, dsts in sends:
-        if held not in waited:
-            waited.add(held)
-            if held == "own":
-                if is_root:
-                    selections_ones()
-                g.wait_ge(T.sem.hq, 1)
-            elif held == "B" and is_root:
-                g.wait_ge(T.sem.bq, 1)
-            else:
-                g.wait_ge(slot_views(held)[2], plan["arrive"][(core, held)])
-        do_send(held, slot, dsts)
+    for held, slot, by in sends:
+        if held == "own":
+            g.wait_ge(T.sem.hq, 1)
+        elif is_root:
+            g.wait_ge(T.sem.bq, 1)
+        do_send(held, slot, by)
+    if is_root:
+        selections_ones()
 
     if rank is not None:
         if is_root:
@@ -209,7 +231,7 @@ def rank_program(g, core, T, topo):
         if is_root:
             g.tensor.wait_ge(T.sem.bq, 1)
         else:
-            g.tensor.wait_ge(T.sem.inb, plan["arrive"][(core, "B")])
+            wait_tile(g.tensor, "B")
         for i in range(4):
             part = slice(W * i, W * i + W)
             g.tensor.matmul_mx(bank(T.pt, i), T.qa[:, part], T.sa[:, part], T.qb[:], T.sb[:], True, True
@@ -223,8 +245,8 @@ def rank_program(g, core, T, topo):
         g.tensor.wait_ge(T.sem.selq, 1)
         slots = plan["gathers"][core]
         for s in slots:
-            codes, scales, sem = slot_views(s)
-            g.tensor.wait_ge(sem, plan["arrive"][(core, s)])
+            codes, scales = slot_views(s)
+            wait_tile(g.tensor, s)
             for b in range(4):
                 part = slice(W * b, W * b + W)
                 mm = g.tensor.matmul_mx(bank(T.ps, b), T.qw[:, part], T.sw[:, part], codes, scales,

@@ -2,6 +2,8 @@ from concourse.bass import DstId, RemoteDMATransfer
 from concourse.mybir import dt, AluOpType, ActivationFunctionType
 
 W = 128
+H = 64
+LAND = 3 * W
 E = 512
 SCRATCH = {
     "bt": ("sbuf", [128, E], "bfloat16"),
@@ -11,18 +13,16 @@ SCRATCH = {
     "qb": ("sbuf", [128, W], "float8_e4m3fn_x4"),
     "sb": ("sbuf", [128, W], "uint8"),
     "wt": ("sbuf", [128, 4 * E], "bfloat16"),
-    "qw": ("sbuf", [128, 4 * W], "float8_e4m3fn_x4"),
-    "sw": ("sbuf", [128, 4 * W], "uint8"),
     "ht": ("sbuf", [128, E], "bfloat16"),
     "qh": ("sbuf", [128, W], "float8_e4m3fn_x4"),
     "sh": ("sbuf", [128, W], "uint8"),
-    "ql": ("sbuf", [128, 4 * W], "float8_e4m3fn_x4"),
-    "sl": ("sbuf", [128, 4 * W], "uint8"),
+    "ql": ("sbuf", [128, LAND + 4 * W], "float8_e4m3fn_x4"),
+    "sl": ("sbuf", [128, LAND + 4 * W], "uint8"),
     "yt": ("sbuf", [128, E], "float32"),
     "pt": ("psum", [128, 2048], "float32"),
     "ps": ("psum", [128, 2048], "float32"),
 }
-SEMAPHORES = (["ldb", "lda", "zed", "dia", "selq", "aq", "bq", "relu", "hq", "cp", "st", "sent", "inb", "scb", "sc0", "sc1"]
+SEMAPHORES = (["ldb", "lda", "zed", "dia", "selq", "aq", "bq", "relu", "hq", "cp", "st", "sent", "inb", "scb", "sc0"]
               + ["in%d" % s for s in range(4)] + ["tm%d" % b for b in range(4)] + ["sm%d" % b for b in range(4)])
 _PLAN = {}
 
@@ -57,64 +57,64 @@ def _plan(T, topo):
     def bits(m):
         return [1 << e for e in range(m.bit_length()) if m >> e & 1]
 
-    def engines(src, dsts, apart):
-        off = [d for d in dsts if not on_chip(src, d)]
-        leaves = [topo.mask(src, d) for d in cores if not on_chip(src, d) and topo.may_write(src, d)][0]
-        by = {}
-        for d in dsts:
-            if on_chip(src, d):
-                m = topo.mask(src, d) & ~leaves
-                if len(off) > 1 and not apart:
-                    m = sum(bits(m)[::2])
-            else:
-                m = topo.mask(src, d)
-                if apart:
-                    share = len(bits(m)) // len(off)
-                    m = sum(bits(m)[share * off.index(d):share * off.index(d) + share])
-            by.setdefault(m, []).append(d)
-        return by
+    leaves = [topo.mask(root, d) for d in cores if topo.may_write(root, d) and not on_chip(root, d)][0]
+    stays = topo.mask(root, [k for k in place[(topo.host(root), topo.chip(root))] if k != root][0]) & ~leaves
 
-    sends, gathers = {}, {}
+    def share(mask, parts, i):
+        e = bits(mask)
+        n = len(e) // parts
+        return sum(e[n * i:n * i + n])
 
-    def send(core, held, slot, dsts, apart=False):
-        sends.setdefault(core, []).append((held, slot, engines(core, dsts, apart)))
+    sends, gathers, arrive, split = {}, {}, {}, set()
+
+    def send(core, held, *transfers):
+        sends.setdefault(core, []).append((held, transfers))
+        for m, lo, n, slot, dsts in transfers:
+            for d in dsts:
+                arrive[(d, slot[0])] = arrive.get((d, slot[0]), 0) + len(bits(m))
+        if held != "own" and core != root:
+            split.add((core, held))
+
+    def whole(m, slot, *dsts):
+        return (m, 0, W, slot, dsts)
 
     far, near = cross(root), root
     far2, near2 = cable(far), cable(near)
-    x0, x1, x2 = helper(near, True), helper(plane(near), True), helper(near2, True)
-    send(root, "B", "B", [x0, x2, plane(root)], apart=True)
-    send(x0, "B", "B", [far, plane(far)])
-    send(x2, "B", "B", [far2, plane(far2), near2])
-    send(plane(root), "B", "B", [cable(plane(root))])
-    summing = {}
-    for c in (far, plane(far), far2, plane(far2)):
-        summing[c] = helper(c, True)
-    for c in (near2, plane(near2)):
-        summing[c] = helper(c, False)
-    both = [summing[far], summing[plane(far)]]
-    for slot, c, x in ((0, root, x0), (1, plane(root), x1)):
-        send(c, "own", slot, [x])
-        send(x, slot, slot, both)
+    B = ("b", 0)
+    x0, xb, x2 = helper(near, True), helper(near, False), helper(near2, True)
+    send(root, "b", whole(stays, B, x0, xb), whole(share(leaves, 2, 0), B, x2), whole(share(leaves, 2, 1), B, plane(root)))
+    send(x0, "b", whole(leaves, B, far, plane(far)))
+    send(xb, "b", whole(leaves, B, far2))
+    send(x2, "b", whole(leaves, B, plane(far2)), whole(stays, B, near2))
+    send(plane(root), "b", whole(leaves, B, cable(plane(root))))
+    adders = {c: [helper(c, True), helper(c, False)] for c in (far, plane(far), far2, plane(far2), near2, plane(near2))}
+
+    def half(m, h, k, chips):
+        return (m, H * h, H, (str(k), W + H * k), [adders[c][h] for c in chips])
+
+    for k, c in ((3, root), (0, plane(root))):
+        xs = [helper(c, True), helper(c, False)]
+        send(c, "own", *[(share(stays, 2, h), H * h, H, ("0", H * h), [xs[h]]) for h in range(2)])
+        for h in range(2):
+            send(xs[h], "0", half(leaves, h, k, [far, plane(far)]))
     for base in (far, far2, near2):
-        for c, own, other in ((base, 2, 3), (plane(base), 3, 2)):
-            send(c, "own", own, [summing[c], summing[plane(c)]])
-            gathers[summing[c]] = [0, own, other, 1] if base == far else [own, other]
-    for c in summing:
-        slot = 0 if rack(c) == rack(root) else (1 if topo.chip(c) == topo.chip(far) else 2)
-        send(summing[c], "own", slot, [c, cross(c), cable(c), cross(cable(c))])
+        for c in (base, plane(base)):
+            here, there = (2, 1) if base == far else (3, 2)
+            send(c, "own", *([half(share(stays, 2, h), h, here, [c]) for h in range(2)]
+                             + [half(share(leaves, 2, h), h, there, [plane(c)]) for h in range(2)]))
+            for h in range(2):
+                gathers[adders[c][h]] = [3, 2, 1, 0] if base == far else [3, 2]
+    for c in adders:
+        tile = 0 if rack(c) == rack(root) else (1 if topo.chip(c) == topo.chip(far) else 2)
+        for h in range(2):
+            slot = (str(tile), W * tile + H * h)
+            send(adders[c][h], "own", (share(stays, 2, 0), 0, H, slot, [c]),
+                 (share(leaves, 2, 0), 0, H, slot, [cross(cable(c)), cable(c)]), (share(leaves, 2, 1), 0, H, slot, [cross(c)]))
     for c in cores:
         side = [1, 2] if topo.chip(c) == topo.chip(far) else [2, 1]
-        gathers[c] = [0] + side if rack(c) == rack(root) else side + [0]
-
-    arrive, split = {}, set()
-    for s in sends:
-        for held, slot, by in sends[s]:
-            if held != "own" and s != root:
-                split.add((s, held))
-            for m in by:
-                for d in by[m]:
-                    arrive[(d, slot)] = len(bits(m))
-    _PLAN.update(root=root, sends=sends, gathers=gathers, arrive=arrive, split=split, summing=set(summing.values()))
+        gathers[c] = [0] + side[::-1] if rack(c) == rack(root) else side + [0]
+    _PLAN.update(root=root, sends=sends, gathers=gathers, arrive=arrive, split=split,
+                 summing=[k for c in adders for k in adders[c]])
     return _PLAN
 
 
@@ -127,15 +127,9 @@ def rank_program(g, core, T, topo):
         return
     sent = [0]
 
-    def slot_views(slot):
-        if slot == "B":
-            return T.qb[:], T.sb[:]
-        return T.ql[:, W * slot:W * slot + W], T.sl[:, W * slot:W * slot + W]
-
     def slot_sems(c, slot):
-        name = str(slot).lower()
-        codes = T.sem["in" + name]
-        return codes, (T.sem["sc" + name] if (c, slot) in plan["split"] else codes)
+        codes = T.sem["in" + slot]
+        return codes, (T.sem["sc" + slot] if (c, slot) in plan["split"] else codes)
 
     def wait_tile(queue, slot):
         n = plan["arrive"][(core, slot)]
@@ -146,29 +140,31 @@ def rank_program(g, core, T, topo):
         else:
             queue.wait_ge(codes, 2 * n)
 
-    def do_send(held, slot, by):
-        if held == "own":
-            codes, scales = T.qh[:], T.sh[:]
-        else:
-            codes, scales = slot_views(held)
-        dcodes, dscales = slot_views(slot)
-        for src, dst, which in ((scales, dscales, 1), (codes.bitcast(dt.uint8), dcodes.bitcast(dt.uint8), 0)):
+    def do_send(held, transfers):
+        for which in (1, 0):
             if (core, held) in plan["split"]:
                 g.wait_ge(slot_sems(core, held)[which], plan["arrive"][(core, held)])
-            transfers = []
-            for m in by:
+            src = {"own": (T.qh, T.sh), "b": (T.qb, T.sb)}.get(held, (T.ql, T.sl))[which]
+            out = []
+            for m, lo, n, (slot, at), dsts in transfers:
                 ids = []
-                for d in by[m]:
+                for d in dsts:
                     rid, pid = topo.addr(d, core)
                     ids.append(DstId(rid=rid, pnc=pid))
-                sem = slot_sems(by[m][0], slot)[which]
-                transfers.append(RemoteDMATransfer(dst_ids=ids, dma_engine_mask=m, remote_sem=sem,
-                                                   srcs=[src], dsts=[dst for d in ids]))
+                land = ((T.qb, T.sb) if slot == "b" else (T.ql, T.sl))[which]
+                piece, spot = src[:, lo:lo + n], land[:, at:at + n]
+                if which == 0:
+                    piece, spot = piece.bitcast(dt.uint8), spot.bitcast(dt.uint8)
+                sem = slot_sems(dsts[0], slot)[which]
+                out.append(RemoteDMATransfer(dst_ids=ids, dma_engine_mask=m, remote_sem=sem,
+                                             srcs=[piece], dsts=[spot for d in ids]))
                 sent[0] += bin(m).count("1")
-            g.remote_dma_fused(transfers, local_sem=T.sem.sent)
+            g.remote_dma_fused(out, local_sem=T.sem.sent)
 
     def selections_zero():
         g.vector.memset(T.wt[:], 0.0).then_inc(T.sem.zed, 1)
+        if sums:
+            g.vector.memset(T.ht[:, 4 * H:], 0.0).then_inc(T.sem.cp, 1)
 
     def selections_ones():
         g.wait_ge(T.sem.zed, 1)
@@ -178,26 +174,26 @@ def rank_program(g, core, T, topo):
 
     def selections_quantise():
         g.vector.wait_ge(T.sem.dia, 4)
-        g.vector.quantize_mx(T.qw[:], T.sw[:], T.wt[:]).then_inc(T.sem.selq, 1)
+        g.vector.quantize_mx(T.ql[:, LAND:LAND + 4 * W], T.sl[:, LAND:LAND + 4 * W], T.wt[:]).then_inc(T.sem.selq, 1)
 
-    def bank(buf, b):
-        return buf[:, 512 * b:512 * b + W]
+    def bank(buf, b, n=W):
+        return buf[:, 512 * b:512 * b + n]
 
-    def drain(buf, mm, out, relu, done):
-        for b in (0, 2):
-            g.vector.wait_ge(T.sem["%s%d" % (mm, b)], 1)
-            v = out[:, b:E:4]
-            if relu:
-                g.vector.tensor_scalar(v, bank(buf, b), 0.0, None, AluOpType.max).then_inc(done, 1)
-            else:
-                g.vector.tensor_copy(v, bank(buf, b)).then_inc(done, 1)
+    def drain(buf, mm, out, n, relu, done):
         for b in (1, 3):
+            g.vector.wait_ge(T.sem["%s%d" % (mm, b)], 1)
+            v = out[:, b:4 * n:4]
+            if relu:
+                g.vector.tensor_scalar(v, bank(buf, b, n), 0.0, None, AluOpType.max).then_inc(done, 1)
+            else:
+                g.vector.tensor_copy(v, bank(buf, b, n)).then_inc(done, 1)
+        for b in (0, 2):
             g.scalar.wait_ge(T.sem["%s%d" % (mm, b)], 1)
             func = ActivationFunctionType.Relu if relu else ActivationFunctionType.Copy
-            g.scalar.activation(out[:, b:E:4], bank(buf, b), func).then_inc(done, 1)
+            g.scalar.activation(out[:, b:4 * n:4], bank(buf, b, n), func).then_inc(done, 1)
 
-    def quantise_own(done):
-        g.vector.wait_ge(done, 4)
+    def quantise_own(done, n):
+        g.vector.wait_ge(done, n)
         g.vector.quantize_mx(T.qh[:], T.sh[:], T.ht[:]).then_inc(T.sem.hq, 1)
 
     if is_root:
@@ -212,12 +208,12 @@ def rank_program(g, core, T, topo):
             selections_ones()
             selections_quantise()
 
-    for held, slot, by in sends:
+    for held, transfers in sends:
         if held == "own":
             g.wait_ge(T.sem.hq, 1)
         elif is_root:
             g.wait_ge(T.sem.bq, 1)
-        do_send(held, slot, by)
+        do_send(held, transfers)
     if is_root:
         selections_ones()
 
@@ -231,13 +227,13 @@ def rank_program(g, core, T, topo):
         if is_root:
             g.tensor.wait_ge(T.sem.bq, 1)
         else:
-            wait_tile(g.tensor, "B")
+            wait_tile(g.tensor, "b")
         for i in range(4):
             part = slice(W * i, W * i + W)
             g.tensor.matmul_mx(bank(T.pt, i), T.qa[:, part], T.sa[:, part], T.qb[:], T.sb[:], True, True
                                ).then_inc(T.sem["tm%d" % i], 1)
-        drain(T.pt, "tm", T.ht, True, T.sem.relu)
-        quantise_own(T.sem.relu)
+        drain(T.pt, "tm", T.ht, W, True, T.sem.relu)
+        quantise_own(T.sem.relu, 4)
         if is_root:
             selections_quantise()
 
@@ -245,19 +241,19 @@ def rank_program(g, core, T, topo):
         g.tensor.wait_ge(T.sem.selq, 1)
         slots = plan["gathers"][core]
         for s in slots:
-            codes, scales = slot_views(s)
-            wait_tile(g.tensor, s)
+            at = W + H * s if sums else W * s
+            wait_tile(g.tensor, str(s))
             for b in range(4):
-                part = slice(W * b, W * b + W)
-                mm = g.tensor.matmul_mx(bank(T.ps, b), T.qw[:, part], T.sw[:, part], codes, scales,
+                sel = slice(LAND + W * b, LAND + W * b + W)
+                mm = g.tensor.matmul_mx(bank(T.ps, b), T.ql[:, sel], T.sl[:, sel], T.ql[:, at:at + W], T.sl[:, at:at + W],
                                         s == slots[0], s == slots[-1])
                 if s == slots[-1]:
                     mm.then_inc(T.sem["sm%d" % b], 1)
         if sums:
-            drain(T.ps, "sm", T.ht, False, T.sem.cp)
-            quantise_own(T.sem.cp)
+            drain(T.ps, "sm", T.ht, H, False, T.sem.cp)
+            quantise_own(T.sem.cp, 5)
         else:
-            drain(T.ps, "sm", T.yt, False, T.sem.cp)
+            drain(T.ps, "sm", T.yt, W, False, T.sem.cp)
             g.sync.wait_ge(T.sem.cp, 4)
             g.sync.dma_start(T.y[:], T.yt[:]).then_inc(T.sem.st, 16)
             g.sync.wait_ge(T.sem.st, 16)

from concourse.bass import DstId, RemoteDMATransfer
from concourse.mybir import dt, AluOpType, ActivationFunctionType

W = 128
H = 64
LAND = 3 * W
E = 512
SCRATCH = {
    "bt": ("sbuf", [128, E], "bfloat16"),
    "at": ("sbuf", [128, 4 * E], "bfloat16"),
    "qa": ("sbuf", [128, 4 * W], "float8_e4m3fn_x4"),
    "sa": ("sbuf", [128, 4 * W], "uint8"),
    "qb": ("sbuf", [128, W], "float8_e4m3fn_x4"),
    "sb": ("sbuf", [128, W], "uint8"),
    "wt": ("sbuf", [128, 4 * E], "bfloat16"),
    "ht": ("sbuf", [128, E], "bfloat16"),
    "qh": ("sbuf", [128, W], "float8_e4m3fn_x4"),
    "sh": ("sbuf", [128, W], "uint8"),
    "ql": ("sbuf", [128, LAND + 4 * W], "float8_e4m3fn_x4"),
    "sl": ("sbuf", [128, LAND + 4 * W], "uint8"),
    "yt": ("sbuf", [128, E], "float32"),
    "pt": ("psum", [128, 2048], "float32"),
    "ps": ("psum", [128, 2048], "float32"),
}
SEMAPHORES = (["ldb", "lda", "zed", "dia", "selq", "aq", "bq", "relu", "hq", "cp", "st", "sent", "inb", "scb", "sc0"]
              + ["in%d" % s for s in range(4)] + ["tm%d" % b for b in range(4)] + ["sm%d" % b for b in range(4)])
_PLAN = {}


def _plan(T, topo):
    if _PLAN:
        return _PLAN
    cores, root = list(T.cores), T.cores[T.root]
    place = {}
    for k in range(512):
        place.setdefault((topo.host(k), topo.chip(k)), []).append(k)

    def cross(c):
        return [d for d in cores if d != c and topo.host(d) == topo.host(c)][0]

    def rack(c):
        return topo.rack(topo.host(c))

    def plane(c):
        return [d for d in cores if d != c and topo.chip(d) == topo.chip(c) and rack(d) == rack(c)][0]

    def cable(c):
        return [d for d in cores if topo.chip(d) == topo.chip(c) and rack(d) != rack(c) and topo.may_write(c, d)][0]

    def helper(c, same_die):
        return [k for k in place[(topo.host(c), topo.chip(c))] if k != c and topo.may_write(k, cross(c))
                and (topo.die(k) == topo.die(c)) == same_die][0]

    def on_chip(src, dst):
        return (topo.host(src), topo.chip(src)) == (topo.host(dst), topo.chip(dst))

    def bits(m):
        return [1 << e for e in range(m.bit_length()) if m >> e & 1]

    leaves = [topo.mask(root, d) for d in cores if topo.may_write(root, d) and not on_chip(root, d)][0]
    stays = topo.mask(root, [k for k in place[(topo.host(root), topo.chip(root))] if k != root][0]) & ~leaves

    def share(mask, parts, i):
        e = bits(mask)
        n = len(e) // parts
        return sum(e[n * i:n * i + n])

    sends, gathers, arrive, split = {}, {}, {}, set()

    def send(core, held, *transfers):
        sends.setdefault(core, []).append((held, transfers))
        for m, lo, n, slot, dsts in transfers:
            for d in dsts:
                arrive[(d, slot[0])] = arrive.get((d, slot[0]), 0) + len(bits(m))
        if held != "own" and core != root:
            split.add((core, held))

    def whole(m, slot, *dsts):
        return (m, 0, W, slot, dsts)

    far, near = cross(root), root
    far2, near2 = cable(far), cable(near)
    B = ("b", 0)
    x0, xb, x2 = helper(near, True), helper(near, False), helper(near2, True)
    send(root, "b", whole(stays, B, x0, xb), whole(share(leaves, 2, 0), B, x2), whole(share(leaves, 2, 1), B, plane(root)))
    send(x0, "b", whole(leaves, B, far, plane(far)))
    send(xb, "b", whole(leaves, B, far2))
    send(x2, "b", whole(leaves, B, plane(far2)), whole(stays, B, near2))
    send(plane(root), "b", whole(leaves, B, cable(plane(root))))
    adders = {c: [helper(c, True), helper(c, False)] for c in (far, plane(far), far2, plane(far2), near2, plane(near2))}

    def half(m, h, k, chips):
        return (m, H * h, H, (str(k), W + H * k), [adders[c][h] for c in chips])

    for k, c in ((3, root), (0, plane(root))):
        xs = [helper(c, True), helper(c, False)]
        send(c, "own", *[(share(stays, 2, h), H * h, H, ("0", H * h), [xs[h]]) for h in range(2)])
        for h in range(2):
            send(xs[h], "0", half(leaves, h, k, [far, plane(far)]))
    for base in (far, far2, near2):
        for c in (base, plane(base)):
            here, there = (2, 1) if base == far else (3, 2)
            send(c, "own", *([half(share(stays, 2, h), h, here, [c]) for h in range(2)]
                             + [half(share(leaves, 2, h), h, there, [plane(c)]) for h in range(2)]))
            for h in range(2):
                gathers[adders[c][h]] = [3, 2, 1, 0] if base == far else [3, 2]
    for c in adders:
        tile = 0 if rack(c) == rack(root) else (1 if topo.chip(c) == topo.chip(far) else 2)
        for h in range(2):
            slot = (str(tile), W * tile + H * h)
            send(adders[c][h], "own", (share(stays, 2, 0), 0, H, slot, [c]),
                 (share(leaves, 2, 0), 0, H, slot, [cross(cable(c)), cable(c)]), (share(leaves, 2, 1), 0, H, slot, [cross(c)]))
    for c in cores:
        side = [1, 2] if topo.chip(c) == topo.chip(far) else [2, 1]
        gathers[c] = [0] + side[::-1] if rack(c) == rack(root) else side + [0]
    _PLAN.update(root=root, sends=sends, gathers=gathers, arrive=arrive, split=split,
                 summing=[k for c in adders for k in adders[c]])
    return _PLAN


def rank_program(g, core, T, topo):
    plan = _plan(T, topo)
    rank = T.rank_of(core)
    sends = plan["sends"].get(core, [])
    is_root, sums = core == plan["root"], core in plan["summing"]
    if rank is None and not sends:
        return
    sent = [0]

    def slot_sems(c, slot):
        codes = T.sem["in" + slot]
        return codes, (T.sem["sc" + slot] if (c, slot) in plan["split"] else codes)

    def wait_tile(queue, slot):
        n = plan["arrive"][(core, slot)]
        codes, scales = slot_sems(core, slot)
        if (core, slot) in plan["split"]:
            queue.wait_ge(scales, n)
            queue.wait_ge(codes, n)
        else:
            queue.wait_ge(codes, 2 * n)

    def do_send(held, transfers):
        for which in (1, 0):
            if (core, held) in plan["split"]:
                g.wait_ge(slot_sems(core, held)[which], plan["arrive"][(core, held)])
            src = {"own": (T.qh, T.sh), "b": (T.qb, T.sb)}.get(held, (T.ql, T.sl))[which]
            out = []
            for m, lo, n, (slot, at), dsts in transfers:
                ids = []
                for d in dsts:
                    rid, pid = topo.addr(d, core)
                    ids.append(DstId(rid=rid, pnc=pid))
                land = ((T.qb, T.sb) if slot == "b" else (T.ql, T.sl))[which]
                piece, spot = src[:, lo:lo + n], land[:, at:at + n]
                if which == 0:
                    piece, spot = piece.bitcast(dt.uint8), spot.bitcast(dt.uint8)
                sem = slot_sems(dsts[0], slot)[which]
                out.append(RemoteDMATransfer(dst_ids=ids, dma_engine_mask=m, remote_sem=sem,
                                             srcs=[piece], dsts=[spot for d in ids]))
                sent[0] += bin(m).count("1")
            g.remote_dma_fused(out, local_sem=T.sem.sent)

    def selections_zero():
        g.vector.memset(T.wt[:], 0.0).then_inc(T.sem.zed, 1)
        if sums:
            g.vector.memset(T.ht[:, 4 * H:], 0.0).then_inc(T.sem.cp, 1)

    def selections_ones():
        g.wait_ge(T.sem.zed, 1)
        for b in range(4):
            v = T.wt[:, E * b + b:E * b + E:4]
            g.affine_select(v, v, [[-1, W]], AluOpType.not_equal, 1.0, 0, 1).then_inc(T.sem.dia, 1)

    def selections_quantise():
        g.vector.wait_ge(T.sem.dia, 4)
        g.vector.quantize_mx(T.ql[:, LAND:LAND + 4 * W], T.sl[:, LAND:LAND + 4 * W], T.wt[:]).then_inc(T.sem.selq, 1)

    def bank(buf, b, n=W):
        return buf[:, 512 * b:512 * b + n]

    def drain(buf, mm, out, n, relu, done):
        for b in (1, 3):
            g.vector.wait_ge(T.sem["%s%d" % (mm, b)], 1)
            v = out[:, b:4 * n:4]
            if relu:
                g.vector.tensor_scalar(v, bank(buf, b, n), 0.0, None, AluOpType.max).then_inc(done, 1)
            else:
                g.vector.tensor_copy(v, bank(buf, b, n)).then_inc(done, 1)
        for b in (0, 2):
            g.scalar.wait_ge(T.sem["%s%d" % (mm, b)], 1)
            func = ActivationFunctionType.Relu if relu else ActivationFunctionType.Copy
            g.scalar.activation(out[:, b:4 * n:4], bank(buf, b, n), func).then_inc(done, 1)

    def quantise_own(done, n):
        g.vector.wait_ge(done, n)
        g.vector.quantize_mx(T.qh[:], T.sh[:], T.ht[:]).then_inc(T.sem.hq, 1)

    if is_root:
        g.sync.dma_start(T.bt[:], T.b[:]).then_inc(T.sem.ldb, 16)
    if rank is not None:
        g.sync.dma_start(T.at[:], T.a[:]).then_inc(T.sem.lda, 16)

    unpacks = rank is not None or sums
    if unpacks:
        selections_zero()
        if not is_root:
            selections_ones()
            selections_quantise()

    for held, transfers in sends:
        if held == "own":
            g.wait_ge(T.sem.hq, 1)
        elif is_root:
            g.wait_ge(T.sem.bq, 1)
        do_send(held, transfers)
    if is_root:
        selections_ones()

    if rank is not None:
        if is_root:
            g.vector.wait_ge(T.sem.ldb, 16)
            g.vector.quantize_mx(T.qb[:], T.sb[:], T.bt[:]).then_inc(T.sem.bq, 1)
        g.vector.wait_ge(T.sem.lda, 16)
        g.vector.quantize_mx(T.qa[:], T.sa[:], T.at[:]).then_inc(T.sem.aq, 1)
        g.tensor.wait_ge(T.sem.aq, 1)
        if is_root:
            g.tensor.wait_ge(T.sem.bq, 1)
        else:
            wait_tile(g.tensor, "b")
        for i in range(4):
            part = slice(W * i, W * i + W)
            g.tensor.matmul_mx(bank(T.pt, i), T.qa[:, part], T.sa[:, part], T.qb[:], T.sb[:], True, True
                               ).then_inc(T.sem["tm%d" % i], 1)
        drain(T.pt, "tm", T.ht, W, True, T.sem.relu)
        quantise_own(T.sem.relu, 4)
        if is_root:
            selections_quantise()

    if unpacks:
        g.tensor.wait_ge(T.sem.selq, 1)
        slots = plan["gathers"][core]
        for s in slots:
            at = W + H * s if sums else W * s
            wait_tile(g.tensor, str(s))
            for b in range(4):
                sel = slice(LAND + W * b, LAND + W * b + W)
                mm = g.tensor.matmul_mx(bank(T.ps, b), T.ql[:, sel], T.sl[:, sel], T.ql[:, at:at + W], T.sl[:, at:at + W],
                                        s == slots[0], s == slots[-1])
                if s == slots[-1]:
                    mm.then_inc(T.sem["sm%d" % b], 1)
        if sums:
            drain(T.ps, "sm", T.ht, H, False, T.sem.cp)
            quantise_own(T.sem.cp, 5)
        else:
            drain(T.ps, "sm", T.yt, W, False, T.sem.cp)
            g.sync.wait_ge(T.sem.cp, 4)
            g.sync.dma_start(T.y[:], T.yt[:]).then_inc(T.sem.st, 16)
            g.sync.wait_ge(T.sem.st, 16)
    if sent[0]:
        g.wait_ge(T.sem.sent, sent[0])
